import numpy as np
import ml_dtypes


def mxq(x, axis, fmt="e4m3"):
    dtype, down = {"e4m3": (ml_dtypes.float8_e4m3fn, 7), "e5m2": (ml_dtypes.float8_e5m2, 14)}[fmt]
    v = np.moveaxis(np.asarray(x, np.float32).astype(ml_dtypes.bfloat16).astype(np.float64), axis, -1)
    blocks = v.reshape(v.shape[:-1] + (-1, 32))
    amax = np.abs(blocks).max(-1, keepdims=True)
    byte = np.maximum(np.where(amax > 0, np.frexp(amax)[1] - 1 + 127, 0) - down, 1)
    scale = np.exp2(byte - 127.0)
    codes = (blocks / scale).astype(np.float32).astype(dtype).astype(np.float64)
    return np.moveaxis((codes * scale).reshape(v.shape), -1, axis)


WIDE = False


def mx_kscale(k):
    if not WIDE:
        return np.ones(k)
    levels = np.array([10, -10, 5, -5, 0])
    if k % 512:
        return np.exp2(np.random.permutation(np.resize(levels, k // 32))).repeat(32)
    a = np.empty((k // 512, 16))
    for p in range(k // 512):
        a[p, :8] = np.random.permutation(np.resize(levels, 8))
        for g in range(8):
            far = levels[np.abs(levels - a[p, g]) >= 10]
            a[p, g + 8] = far[np.random.randint(len(far))]
    return np.exp2(a.ravel()).repeat(32)


def f64(x):
    return np.asarray(x).astype(np.float64)


def striped(idx):
    return np.tile(idx.reshape(-1, 16).T, (8, 1)).astype(np.uint16)


def unstriped(offs):
    return offs[:16].T.reshape(-1).astype(np.int64)


E2M1 = np.array([0.0, 0.5, 1.0, 1.5, 2.0, 3.0, 4.0, 6.0, -0.0, -0.5, -1.0, -1.5, -2.0, -3.0, -4.0, -6.0])


def pack_weight(w, fmt):
    k, n = w.shape
    w = f64(np.asarray(w, np.float32).astype(ml_dtypes.bfloat16)).reshape(k // 32, 32, n)
    amax = np.abs(w).max(1)
    if fmt == "e4m3":
        byte = np.frexp(amax)[1] - 1 + 127 - 7
    else:
        mant, ex = np.frexp(amax / 6.0)
        byte = np.where(mant > 0.5, ex, ex - 1) + 127
    byte = np.clip(np.where(amax > 0, byte, 1), 1, 254)
    scaled = (w * np.exp2(127.0 - byte)[:, None, :]).reshape(k, n).astype(np.float32)
    by_word = np.ascontiguousarray(scaled.reshape(k // 512, 128, 4, n).transpose(0, 1, 3, 2))
    if fmt == "e4m3":
        words = by_word.astype(ml_dtypes.float8_e4m3fn).view(np.uint8)
    else:
        c = by_word.astype(ml_dtypes.float4_e2m1fn).view(np.uint8) & 0xF
        words = (c[..., 0::2] | (c[..., 1::2] << 4)).reshape(k // 512, 128, 2 * n)
    return np.ascontiguousarray(words), np.ascontiguousarray(byte.astype(np.uint8).reshape(k // 512, 16, n))


def unpack_weight(words, scales, fmt):
    g, _, n = scales.shape
    words = np.ascontiguousarray(words).reshape(g, 128, n, -1)
    if fmt == "e4m3":
        vals = words.view(ml_dtypes.float8_e4m3fn).astype(np.float64)
    else:
        nib = np.empty((g, 128, n, 4), np.uint8)
        nib[..., 0::2] = words & 0xF
        nib[..., 1::2] = words >> 4
        vals = E2M1[nib]
    vals = vals * np.repeat(np.exp2(scales.astype(np.float64) - 127.0), 8, axis=1)[..., None]
    return vals.transpose(0, 1, 3, 2).reshape(g * 512, n)


def gelu(v):
    return 0.5 * v * (1.0 + np.tanh(np.sqrt(2.0 / np.pi) * (v + 0.044715 * v**3)))


K, T, S, H, P, N = 1024, 4096, 1024, 1024, 512, 512


def setup_inputs():
    n = np.random.standard_normal
    s = mx_kscale(K)[:, None]
    u = mx_kscale(H)[:, None]
    d = {}
    d["tab_words"], d["tab_scales"] = pack_weight(n((K, T)) * s, "e2m1")
    d["offs"] = striped(np.random.permutation(T)[:S])
    d["pos1"] = striped(np.random.permutation(S)[:P])
    d["pos2"] = striped(np.random.permutation(S)[:P])
    d["w1"] = (0.54 * n((K, H)) / K ** 0.5 / s).astype(np.float32)
    d["gain"] = (1.8 * np.exp(0.3 * n(H)) * u[:, 0]).astype(np.float32)
    d["ecc"] = (0.6 * n((H, P)) * u).astype(np.float32)
    w2 = n((H, N)) * np.exp(0.4 * n((1, N))) / H ** 0.5 / u
    d["w2_words"], d["w2_scales"] = pack_weight(w2, "e2m1")
    return d


def reference(tab_words, tab_scales, offs, pos1, pos2, w1, gain, ecc, w2_words, w2_scales):
    v = unpack_weight(tab_words, tab_scales, "e2m1")[:, unstriped(offs)]
    raw = mxq(f64(w1), 0, "e4m3").T @ v
    h = f64(gain)[:, None] * raw
    near = h[:, unstriped(pos1)]
    turn = np.cos(raw[:, unstriped(pos2)])
    x = near * turn + f64(ecc)
    w2 = unpack_weight(w2_words, w2_scales, "e2m1")
    y = w2.T @ mxq(x, 0, "e4m3")
    return np.sqrt(np.abs(y) + 0.2)

@@ -1,0 +1,298 @@
+import math
+from contextlib import ExitStack
+
+import concourse.mybir as mybir
+
+K, T, S, H, PAIRS, N = 1024, 4096, 1024, 1024, 512, 512
+FLOPS = 2 * K * H * S + 2 * H * N * PAIRS
+
+F32 = mybir.dt.float32
+BF16 = mybir.dt.bfloat16
+I32 = mybir.dt.int32
+U32 = mybir.dt.uint32
+U16 = mybir.dt.uint16
+U8 = mybir.dt.uint8
+FP8X4 = mybir.dt.float8_e4m3fn_x4
+FP4X4 = mybir.dt.float4_e2m1fn_x4
+ALU = mybir.AluOpType
+ACT = mybir.ActivationFunctionType
+
+P = 128
+PACK = 4
+K_PASS = P * PACK
+BANK = 512
+WINDOW = 2 * S
+WINDOWS = 6
+ROUNDER = 1.5 * 2.0**23
+PIECES = [(0, 256), (256, 256)]
+CAST_ON_VECTOR = [[0, 80], [32, 32]]
+
+
+def tile_list_groove_crosstalk_scores_kernel(
+    tc, tab_words, tab_scales, offs, pos1, pos2, w1, gain, ecc, w2_words, w2_scales, out
+):
+    nc = tc.nc
+    with ExitStack() as ctx:
+        lists = ctx.enter_context(tc.tile_pool(name="lists", bufs=1))
+        keep = ctx.enter_context(tc.tile_pool(name="keep", bufs=1))
+        ring = ctx.enter_context(tc.tile_pool(name="ring", bufs=3))
+        stage = ctx.enter_context(tc.tile_pool(name="stage", bufs=2))
+        psum1 = ctx.enter_context(tc.psum_pool(name="psum1", bufs=4))
+        psum2 = ctx.enter_context(tc.psum_pool(name="psum2", bufs=1))
+
+        offs_t = lists.tile([P, S // 16], U16, name="offs_t")
+        pos1_t = lists.tile([P, PAIRS // 16], U16, name="pos1_t")
+        pos2_t = lists.tile([P, PAIRS // 16], U16, name="pos2_t")
+
+        tab_w = [keep.tile([P, T], U16, name="tab_w%d" % a) for a in range(2)]
+        tab_s = keep.tile([P, T], U8, name="tab_s")
+        v_words = [keep.tile([P, S], U16, name="v_words%d" % a, align_bytes=64) for a in range(2)]
+        v_scales = [keep.tile([P, S], U8, name="v_scales%d" % a, align_bytes=64) for a in range(2)]
+        w_raw = {}
+        w_bf = {}
+        w_codes = {}
+        w_scales = {}
+        for b in range(2):
+            for a in range(2):
+                w_bf[b, a] = keep.tile([P, PACK, P, PACK], BF16, name="w_bf%d%d" % (b, a), align_bytes=64)
+                w_codes[b, a] = keep.tile([P, K_PASS], U32, name="w_codes%d%d" % (b, a), align_bytes=64)
+                w_scales[b, a] = keep.tile([P, K_PASS], U8, name="w_scales%d%d" % (b, a), align_bytes=64)
+        windows = [keep.tile([P, WINDOW], F32, name="window%d" % i) for i in range(WINDOWS)]
+        gain_t = keep.tile([P, 2, PACK], F32, name="gain_t")
+        ecc_t = {}
+        x_bf = [keep.tile([P, PACK, PAIRS], BF16, name="x_bf%d" % b) for b in range(2)]
+        turns = [keep.tile([P, PAIRS], F32, name="turn%d" % i) for i in range(8)]
+        zero_in = keep.tile([P, 1], F32, name="zero_in")
+        zero_bias = keep.tile([P, 1], F32, name="zero_bias")
+
+        half = T // 8
+        nc.vector.memset(tab_s[:].bitcast(I32)[:, 0:half], 0)
+        nc.gpsimd.memset(tab_s[:].bitcast(I32)[:, half : 2 * half], 0)
+        nc.gpsimd.memset(zero_in[:], 0.0)
+        nc.scalar.activation(zero_bias[:], zero_in[:], ACT.Sin)
+        nc.gpsimd.memset(v_scales[1][:].bitcast(I32), 0)
+
+        def load_w1(b, a):
+            rows = w1[a * K_PASS : (a + 1) * K_PASS, b * K_PASS : (b + 1) * K_PASS]
+            w_raw[b, a] = stage.tile([P, PACK, K_PASS], F32, name="staged")
+            nc.sync.dma_start(out=w_raw[b, a][:], in_=rows.rearrange("(p j) c -> p j c", j=PACK))
+
+        def load_ecc(b):
+            rows = ecc[b * K_PASS : (b + 1) * K_PASS, :]
+            if b == 0:
+                ecc_t[b] = keep.tile([P, PACK, PAIRS], F32, name="tab_w1")
+            else:
+                ecc_t[b] = stage.tile([P, PACK, PAIRS], F32, name="staged")
+            nc.sync.dma_start(out=ecc_t[b][:], in_=rows.rearrange("(p t) m -> p t m", t=PACK))
+
+        nc.sync.dma_start(offs_t[:], offs)
+        nc.sync.dma_start(out=tab_w[0][:].bitcast(I32), in_=tab_words[0].bitcast(I32))
+        for q in range(4):
+            nc.gpsimd.dma_start(
+                out=tab_s[32 * q : 32 * q + 8, :].bitcast(I32),
+                in_=tab_scales[:, 4 * q : 4 * q + 4, :].bitcast(I32),
+            )
+        load_w1(0, 0)
+        nc.sync.dma_start(out=tab_w[1][:].bitcast(I32), in_=tab_words[1].bitcast(I32))
+        load_w1(0, 1)
+        nc.sync.dma_start(pos2_t[:], pos2)
+        nc.sync.dma_start(pos1_t[:], pos1)
+        nc.sync.dma_start(out=gain_t[:], in_=gain.rearrange("(b p t) -> p b t", b=2, t=PACK))
+
+        def cast_w1(b, a, lo, hi, on_vector):
+            if hi <= lo:
+                return
+            dst = w_bf[b, a][:].rearrange("p t m j -> p m t j")[:, lo:hi, :, :]
+            src = w_raw[b, a][:].rearrange("p j (m t) -> p m t j", t=PACK)[:, lo:hi, :, :]
+            if on_vector:
+                nc.vector.tensor_copy(out=dst, in_=src)
+            else:
+                nc.scalar.copy(out=dst, in_=src)
+
+        def quantize_w1(b, a, parts):
+            flat = w_bf[b, a][:].rearrange("p t m j -> p (t m j)")
+            step = K_PASS // parts
+            for c in range(0, K_PASS, step):
+                nc.vector.quantize_mx(
+                    out=w_codes[b, a][:, c : c + step].bitcast(FP8X4),
+                    scales=w_scales[b, a][:, c : c + step],
+                    in_=flat[:, PACK * c : PACK * (c + step)],
+                )
+
+        def cast_both(b, a):
+            split = P - CAST_ON_VECTOR[b][a]
+            cast_w1(b, a, 0, split // 2, False)
+            cast_w1(b, a, split // 2, split, False)
+            cast_w1(b, a, split, P, True)
+
+        nc.vector.tensor_copy(out=v_words[0][:], in_=tab_w[0][:].indirect(offs_t[:]))
+        nc.vector.tensor_copy(out=v_scales[0][:], in_=tab_s[:].indirect(offs_t[:]))
+        nc.sync.dma_start(out=v_scales[1][0:112, :].bitcast(I32), in_=v_scales[0][4:116, :].bitcast(I32))
+        cast_both(0, 0)
+        nc.vector.tensor_copy(out=v_words[1][:], in_=tab_w[1][:].indirect(offs_t[:]))
+        load_w1(1, 0)
+        load_ecc(0)
+        quantize_w1(0, 0, 1)
+        cast_both(0, 1)
+        load_w1(1, 1)
+        quantize_w1(0, 1, 4)
+        w2_w = keep.tile([P, 2, 2 * N], U8, name="w_bf00", align_bytes=64)
+        w2_s = keep.tile([P, 2, N], U8, name="w_bf01", align_bytes=64)
+        nc.gpsimd.memset(w2_s[:].rearrange("p a n -> p (a n)").bitcast(I32), 0)
+        nc.sync.dma_start(out=w2_w[:].bitcast(I32), in_=w2_words.rearrange("a p c -> p a c").bitcast(I32))
+        for q in range(4):
+            nc.sync.dma_start(
+                out=w2_s[32 * q : 32 * q + 4, :, :].bitcast(I32),
+                in_=w2_scales[:, 4 * q : 4 * q + 4, :].rearrange("a r c -> r a c").bitcast(I32),
+            )
+
+        phase = {}
+        whole = {}
+
+        def first_product(i):
+            b, t = divmod(i, PACK)
+            cols = slice(t * P, (t + 1) * P)
+            for h in range(2):
+                bank = psum1.tile([P, BANK], F32, name="bank")
+                for a in range(2):
+                    nc.tensor.matmul_mx(
+                        out=bank[:],
+                        lhsT=w_codes[b, a][:, cols].bitcast(FP8X4),
+                        lhsT_scale=w_scales[b, a][:, cols],
+                        rhs=v_words[a][:, h * BANK : (h + 1) * BANK].bitcast(FP4X4),
+                        rhs_scale=v_scales[a][:, h * BANK : (h + 1) * BANK],
+                        start=(a == 0),
+                        stop=(a == 1),
+                    )
+                dst = windows[i % WINDOWS][:, h * BANK : (h + 1) * BANK]
+                if (i, h) in [(0, 1)]:
+                    nc.vector.tensor_copy(out=dst, in_=bank[:])
+                else:
+                    nc.scalar.copy(out=dst, in_=bank[:])
+
+        def pick_phase(i):
+            phase[i] = ring.tile([P, PAIRS], F32, name="phase")
+            nc.vector.tensor_scalar(
+                out=phase[i][:],
+                in0=windows[i % WINDOWS][:].indirect(pos2_t[:]),
+                scalar1=1.0 / (2.0 * math.pi),
+                scalar2=0.25,
+                op0=ALU.mult,
+                op1=ALU.add,
+            )
+            whole[i] = ring.tile([P, PAIRS], U32, name="whole")
+            nc.scalar.activation(whole[i][:], phase[i][:], ACT.Copy, bias=ROUNDER, scale=1.0)
+
+        def cosine(i):
+            rest = ring.tile([P, PAIRS], F32, name="rest")
+            nc.vector.scalar_tensor_tensor(
+                out=rest[:],
+                in0=whole[i][:].bitcast(I32),
+                scalar=ROUNDER,
+                in1=phase[i][:],
+                op0=ALU.subtract,
+                op1=ALU.subtract,
+            )
+            nc.scalar.activation(turns[i][:], rest[:], ACT.Sin, bias=zero_bias[:], scale=-2.0 * math.pi)
+
+        def combine(i, m0, width):
+            b, t = divmod(i, PACK)
+            prod = ring.tile([P, width], F32, name="prod")
+            if width == PAIRS:
+                picks = pos1_t[:]
+            else:
+                picks = pos1_t[:, m0 // 16 : (m0 + width) // 16]
+            nc.vector.tensor_tensor(
+                out=prod[:], in0=windows[i % WINDOWS][:].indirect(picks), in1=turns[i][:, m0 : m0 + width], op=ALU.mult
+            )
+            nc.vector.scalar_tensor_tensor(
+                out=x_bf[b][:, t, m0 : m0 + width],
+                in0=prod[:],
+                scalar=gain_t[:, b, t : t + 1],
+                in1=ecc_t[b][:, t, m0 : m0 + width],
+                op0=ALU.mult,
+                op1=ALU.add,
+            )
+
+        x_codes = {}
+        x_scales = {}
+
+        def quantize_x(b, m0, width, on_vector):
+            woven = keep.tile([P, width, PACK], BF16, name="woven%d_%d" % (b, m0), align_bytes=64)
+            dst = woven[:].rearrange("p (c i) t -> p c t i", i=4)
+            src = x_bf[b][:, :, m0 : m0 + width].rearrange("p t (c i) -> p c t i", i=4)
+            if on_vector:
+                nc.vector.tensor_copy(out=dst, in_=src)
+            else:
+                nc.scalar.copy(out=dst, in_=src)
+            x_codes[b, m0] = keep.tile([P, width], U32, name="x_codes%d_%d" % (b, m0), align_bytes=64)
+            x_scales[b, m0] = keep.tile([P, width], U8, name="x_scales%d_%d" % (b, m0), align_bytes=64)
+            nc.vector.quantize_mx(
+                out=x_codes[b, m0][:].bitcast(FP8X4),
+                scales=x_scales[b, m0][:],
+                in_=woven[:].rearrange("p m t -> p (m t)"),
+            )
+
+        sums = {}
+
+        def second_product(b, m0, width, base):
+            per_bank = BANK // width
+            for n0 in range(0, N // P, per_bank):
+                if b == 0:
+                    sums[m0, n0] = psum2.tile([P, per_bank, width], F32, name="sums%d_%d" % (m0, n0))
+                steps = [(n, c) for n in range(per_bank) for c in range(0, width, P)]
+                for n, c in steps:
+                    cols = slice(m0 - base + c, m0 - base + c + P)
+                    nc.tensor.matmul_mx(
+                        out=sums[m0, n0][:, n, c : c + P],
+                        lhsT=w2_w[:, b, 2 * P * (n0 + n) : 2 * P * (n0 + n + 1)].bitcast(FP4X4),
+                        lhsT_scale=w2_s[:, b, P * (n0 + n) : P * (n0 + n + 1)],
+                        rhs=x_codes[b, base][:, cols].bitcast(FP8X4),
+                        rhs_scale=x_scales[b, base][:, cols],
+                        start=(b == 0 and (n, c) == steps[0]),
+                        stop=(b == 1 and (n, c) == steps[-1]),
+                    )
+
+        out_rows = out.rearrange("(n p) m -> p n m", p=P)
+
+        def finish(m0, width):
+            per_bank = BANK // width
+            for n0 in range(0, N // P, per_bank):
+                size = ring.tile([P, per_bank, width], F32, name="size")
+                nc.scalar.activation(size[:], sums[m0, n0][:], ACT.Abs)
+                score = ring.tile([P, per_bank, width], F32, name="score")
+                nc.scalar.activation(score[:], size[:], ACT.Sqrt, bias=0.2)
+                nc.sync.dma_start(out=out_rows[:, n0 : n0 + per_bank, m0 : m0 + width], in_=score[:])
+
+        first_m0, first_width = PIECES[0]
+        first_product(0)
+        first_product(1)
+        for s in range(10):
+            if s < 8:
+                pick_phase(s)
+            if s + 2 < 8:
+                if s + 2 == 4:
+                    quantize_w1(1, 0, 1)
+                    quantize_w1(1, 1, 1)
+                first_product(s + 2)
+            if s < 2:
+                cast_both(1, s)
+            if s == 0:
+                load_ecc(1)
+            if 1 <= s < 9:
+                cosine(s - 1)
+            if 2 <= s < 6:
+                combine(s - 2, 0, PAIRS)
+            if s == 6:
+                quantize_x(0, 0, PAIRS, False)
+                for m0, width in PIECES:
+                    second_product(0, m0, width, 0)
+            if s >= 6:
+                combine(s - 2, first_m0, first_width)
+        for k, (m0, width) in enumerate(PIECES):
+            if k > 0:
+                for i in range(4, 8):
+                    combine(i, m0, width)
+            quantize_x(1, m0, width, True)
+            second_product(1, m0, width, m0)
+            finish(m0, width)

@@ -24,8 +24,9 @@ BANK = 512
 WINDOW = 2 * S
 WINDOWS = 6
 ROUNDER = 1.5 * 2.0**23
-PIECES = [(0, 256), (256, 256)]
-CAST_ON_VECTOR = [[0, 80], [32, 32]]
+HALF = PAIRS // 2
+PIECES = [(0, 256), (256, 128), (384, 128)]
+CAST_ON_VECTOR = [[32, 64], [48, 0]]
 
 
 def tile_list_groove_crosstalk_scores_kernel(
@@ -36,7 +37,7 @@ def tile_list_groove_crosstalk_scores_kernel(
         lists = ctx.enter_context(tc.tile_pool(name="lists", bufs=1))
         keep = ctx.enter_context(tc.tile_pool(name="keep", bufs=1))
         ring = ctx.enter_context(tc.tile_pool(name="ring", bufs=3))
-        stage = ctx.enter_context(tc.tile_pool(name="stage", bufs=2))
+        pair = ctx.enter_context(tc.tile_pool(name="pair", bufs=2))
         psum1 = ctx.enter_context(tc.psum_pool(name="psum1", bufs=4))
         psum2 = ctx.enter_context(tc.psum_pool(name="psum2", bufs=1))
 
@@ -44,10 +45,11 @@ def tile_list_groove_crosstalk_scores_kernel(
         pos1_t = lists.tile([P, PAIRS // 16], U16, name="pos1_t")
         pos2_t = lists.tile([P, PAIRS // 16], U16, name="pos2_t")
 
-        tab_w = [keep.tile([P, T], U16, name="tab_w%d" % a) for a in range(2)]
+        tab_w = [keep.tile([P, T], U16, name="slot_tab%d" % a) for a in range(2)]
         tab_s = keep.tile([P, T], U8, name="tab_s")
+        picked_s = keep.tile([P, S], U8, name="picked_s")
         v_words = [keep.tile([P, S], U16, name="v_words%d" % a, align_bytes=64) for a in range(2)]
-        v_scales = [keep.tile([P, S], U8, name="v_scales%d" % a, align_bytes=64) for a in range(2)]
+        v_scales = keep.tile([P, 2, S], U8, name="v_scales", align_bytes=64)
         w_raw = {}
         w_bf = {}
         w_codes = {}
@@ -58,50 +60,37 @@ def tile_list_groove_crosstalk_scores_kernel(
                 w_codes[b, a] = keep.tile([P, K_PASS], U32, name="w_codes%d%d" % (b, a), align_bytes=64)
                 w_scales[b, a] = keep.tile([P, K_PASS], U8, name="w_scales%d%d" % (b, a), align_bytes=64)
         windows = [keep.tile([P, WINDOW], F32, name="window%d" % i) for i in range(WINDOWS)]
-        gain_t = keep.tile([P, 2, PACK], F32, name="gain_t")
         ecc_t = {}
-        x_bf = [keep.tile([P, PACK, PAIRS], BF16, name="x_bf%d" % b) for b in range(2)]
         turns = [keep.tile([P, PAIRS], F32, name="turn%d" % i) for i in range(8)]
         zero_in = keep.tile([P, 1], F32, name="zero_in")
         zero_bias = keep.tile([P, 1], F32, name="zero_bias")
 
-        half = T // 8
-        nc.vector.memset(tab_s[:].bitcast(I32)[:, 0:half], 0)
-        nc.gpsimd.memset(tab_s[:].bitcast(I32)[:, half : 2 * half], 0)
+        nc.vector.memset(tab_s[64:128, :].bitcast(I32), 0)
         nc.gpsimd.memset(zero_in[:], 0.0)
+        nc.gpsimd.memset(tab_s[32:64, :].bitcast(I32), 0)
         nc.scalar.activation(zero_bias[:], zero_in[:], ACT.Sin)
-        nc.gpsimd.memset(v_scales[1][:].bitcast(I32), 0)
+        nc.gpsimd.memset(v_scales[:].rearrange("p a s -> p (a s)").bitcast(I32), 0)
 
-        def load_w1(b, a):
+        def load_w1(b, a, slot):
             rows = w1[a * K_PASS : (a + 1) * K_PASS, b * K_PASS : (b + 1) * K_PASS]
-            w_raw[b, a] = stage.tile([P, PACK, K_PASS], F32, name="staged")
+            w_raw[b, a] = keep.tile([P, PACK, K_PASS], F32, name=slot)
             nc.sync.dma_start(out=w_raw[b, a][:], in_=rows.rearrange("(p j) c -> p j c", j=PACK))
 
-        def load_ecc(b):
+        def load_ecc(b, slot):
             rows = ecc[b * K_PASS : (b + 1) * K_PASS, :]
-            if b == 0:
-                ecc_t[b] = keep.tile([P, PACK, PAIRS], F32, name="tab_w1")
-            else:
-                ecc_t[b] = stage.tile([P, PACK, PAIRS], F32, name="staged")
+            ecc_t[b] = keep.tile([P, PACK, PAIRS], F32, name=slot)
             nc.sync.dma_start(out=ecc_t[b][:], in_=rows.rearrange("(p t) m -> p t m", t=PACK))
 
         nc.sync.dma_start(offs_t[:], offs)
+        nc.sync.dma_start(out=tab_s[0:32, :].bitcast(I32), in_=tab_scales.rearrange("a g c -> g a c").bitcast(I32))
         nc.sync.dma_start(out=tab_w[0][:].bitcast(I32), in_=tab_words[0].bitcast(I32))
-        for q in range(4):
-            nc.gpsimd.dma_start(
-                out=tab_s[32 * q : 32 * q + 8, :].bitcast(I32),
-                in_=tab_scales[:, 4 * q : 4 * q + 4, :].bitcast(I32),
-            )
-        load_w1(0, 0)
+        load_w1(0, 0, "slot_w0")
         nc.sync.dma_start(out=tab_w[1][:].bitcast(I32), in_=tab_words[1].bitcast(I32))
-        load_w1(0, 1)
+        load_w1(0, 1, "slot_w1")
         nc.sync.dma_start(pos2_t[:], pos2)
         nc.sync.dma_start(pos1_t[:], pos1)
-        nc.sync.dma_start(out=gain_t[:], in_=gain.rearrange("(b p t) -> p b t", b=2, t=PACK))
 
         def cast_w1(b, a, lo, hi, on_vector):
-            if hi <= lo:
-                return
             dst = w_bf[b, a][:].rearrange("p t m j -> p m t j")[:, lo:hi, :, :]
             src = w_raw[b, a][:].rearrange("p j (m t) -> p m t j", t=PACK)[:, lo:hi, :, :]
             if on_vector:
@@ -123,23 +112,28 @@ def tile_list_groove_crosstalk_scores_kernel(
             split = P - CAST_ON_VECTOR[b][a]
             cast_w1(b, a, 0, split // 2, False)
             cast_w1(b, a, split // 2, split, False)
-            cast_w1(b, a, split, P, True)
+            if split < P:
+                cast_w1(b, a, split, P, True)
 
+        nc.vector.tensor_copy(out=picked_s[:], in_=tab_s[:].indirect(offs_t[:]))
+        for q in range(4):
+            nc.scalar.dma_start(
+                out=v_scales[32 * q : 32 * q + 4, :, :].bitcast(I32),
+                in_=picked_s[8 * q : 8 * q + 8, :].bitcast(I32),
+            )
         nc.vector.tensor_copy(out=v_words[0][:], in_=tab_w[0][:].indirect(offs_t[:]))
-        nc.vector.tensor_copy(out=v_scales[0][:], in_=tab_s[:].indirect(offs_t[:]))
-        nc.sync.dma_start(out=v_scales[1][0:112, :].bitcast(I32), in_=v_scales[0][4:116, :].bitcast(I32))
+        load_w1(1, 0, "slot_tab0")
         cast_both(0, 0)
+        gain_t = keep.tile([P, 2, PACK], F32, name="slot_w0")
+        nc.sync.dma_start(out=gain_t[:], in_=gain.rearrange("(b p t) -> p b t", b=2, t=PACK))
         nc.vector.tensor_copy(out=v_words[1][:], in_=tab_w[1][:].indirect(offs_t[:]))
-        load_w1(1, 0)
-        load_ecc(0)
+        load_ecc(0, "slot_tab1")
         quantize_w1(0, 0, 1)
         cast_both(0, 1)
-        load_w1(1, 1)
-        quantize_w1(0, 1, 4)
-        w2_w = keep.tile([P, 2, 2 * N], U8, name="w_bf00", align_bytes=64)
+        load_w1(1, 1, "slot_w1")
+        quantize_w1(0, 1, 1)
         w2_s = keep.tile([P, 2, N], U8, name="w_bf01", align_bytes=64)
         nc.gpsimd.memset(w2_s[:].rearrange("p a n -> p (a n)").bitcast(I32), 0)
-        nc.sync.dma_start(out=w2_w[:].bitcast(I32), in_=w2_words.rearrange("a p c -> p a c").bitcast(I32))
         for q in range(4):
             nc.sync.dma_start(
                 out=w2_s[32 * q : 32 * q + 4, :, :].bitcast(I32),
@@ -160,7 +154,7 @@ def tile_list_groove_crosstalk_scores_kernel(
                         lhsT=w_codes[b, a][:, cols].bitcast(FP8X4),
                         lhsT_scale=w_scales[b, a][:, cols],
                         rhs=v_words[a][:, h * BANK : (h + 1) * BANK].bitcast(FP4X4),
-                        rhs_scale=v_scales[a][:, h * BANK : (h + 1) * BANK],
+                        rhs_scale=v_scales[:, a, h * BANK : (h + 1) * BANK],
                         start=(a == 0),
                         stop=(a == 1),
                     )
@@ -195,19 +189,23 @@ def tile_list_groove_crosstalk_scores_kernel(
             )
             nc.scalar.activation(turns[i][:], rest[:], ACT.Sin, bias=zero_bias[:], scale=-2.0 * math.pi)
 
-        def combine(i, m0, width):
-            b, t = divmod(i, PACK)
-            prod = ring.tile([P, width], F32, name="prod")
+        def pick_product(i, prod, m0, width):
             if width == PAIRS:
                 picks = pos1_t[:]
             else:
                 picks = pos1_t[:, m0 // 16 : (m0 + width) // 16]
             nc.vector.tensor_tensor(
-                out=prod[:], in0=windows[i % WINDOWS][:].indirect(picks), in1=turns[i][:, m0 : m0 + width], op=ALU.mult
+                out=prod[:, i % PACK, :],
+                in0=windows[i % WINDOWS][:].indirect(picks),
+                in1=turns[i][:, m0 : m0 + width],
+                op=ALU.mult,
             )
+
+        def add_offsets(i, prod, x_rows, m0, width):
+            b, t = divmod(i, PACK)
             nc.vector.scalar_tensor_tensor(
-                out=x_bf[b][:, t, m0 : m0 + width],
-                in0=prod[:],
+                out=x_rows[:, t, :],
+                in0=prod[:, t, :],
                 scalar=gain_t[:, b, t : t + 1],
                 in1=ecc_t[b][:, t, m0 : m0 + width],
                 op0=ALU.mult,
@@ -217,10 +215,10 @@ def tile_list_groove_crosstalk_scores_kernel(
         x_codes = {}
         x_scales = {}
 
-        def quantize_x(b, m0, width, on_vector):
-            woven = keep.tile([P, width, PACK], BF16, name="woven%d_%d" % (b, m0), align_bytes=64)
+        def quantize_x(b, x_rows, rows_m0, m0, width, on_vector):
+            woven = keep.tile([P, width, PACK], BF16, name="woven%d" % width, align_bytes=64)
             dst = woven[:].rearrange("p (c i) t -> p c t i", i=4)
-            src = x_bf[b][:, :, m0 : m0 + width].rearrange("p t (c i) -> p c t i", i=4)
+            src = x_rows[:, :, m0 - rows_m0 : m0 - rows_m0 + width].rearrange("p t (c i) -> p c t i", i=4)
             if on_vector:
                 nc.vector.tensor_copy(out=dst, in_=src)
             else:
@@ -258,41 +256,53 @@ def tile_list_groove_crosstalk_scores_kernel(
         def finish(m0, width):
             per_bank = BANK // width
             for n0 in range(0, N // P, per_bank):
-                size = ring.tile([P, per_bank, width], F32, name="size")
-                nc.scalar.activation(size[:], sums[m0, n0][:], ACT.Abs)
+                size = pair.tile([P, per_bank, width], F32, name="size")
+                nc.scalar.activation(size[:], sums[m0, n0][:], ACT.Abs, bias=zero_late[:])
                 score = ring.tile([P, per_bank, width], F32, name="score")
                 nc.scalar.activation(score[:], size[:], ACT.Sqrt, bias=0.2)
                 nc.sync.dma_start(out=out_rows[:, n0 : n0 + per_bank, m0 : m0 + width], in_=score[:])
 
-        first_m0, first_width = PIECES[0]
+        prod_full = keep.tile([P, PACK, PAIRS], F32, name="prod_full")
+        x_full = keep.tile([P, PACK, PAIRS], BF16, name="x_full")
+        prod_half = keep.tile([P, PACK, HALF], F32, name="prod_half")
+        x_half = [keep.tile([P, PACK, HALF], BF16, name="x_half%d" % h) for h in range(2)]
         first_product(0)
         first_product(1)
-        for s in range(10):
+        for s in range(9):
             if s < 8:
                 pick_phase(s)
+            if s >= 1:
+                i = s - 1
+                cosine(i)
+                if i < PACK:
+                    pick_product(i, prod_full, 0, PAIRS)
+                    add_offsets(i, prod_full, x_full, 0, PAIRS)
+                else:
+                    pick_product(i, prod_half, 0, HALF)
+                    add_offsets(i, prod_half, x_half[0], 0, HALF)
+            if s in (1, 2):
+                cast_both(1, s - 1)
+                quantize_w1(1, s - 1, 1)
+            if s == 1:
+                load_ecc(1, "slot_tab0")
+                w2_w = keep.tile([P, 2, 2 * N], U8, name="w_bf10", align_bytes=64)
+                nc.sync.dma_start(out=w2_w[:].bitcast(I32), in_=w2_words.rearrange("a p c -> p a c").bitcast(I32))
             if s + 2 < 8:
-                if s + 2 == 4:
-                    quantize_w1(1, 0, 1)
-                    quantize_w1(1, 1, 1)
                 first_product(s + 2)
-            if s < 2:
-                cast_both(1, s)
-            if s == 0:
-                load_ecc(1)
-            if 1 <= s < 9:
-                cosine(s - 1)
-            if 2 <= s < 6:
-                combine(s - 2, 0, PAIRS)
-            if s == 6:
-                quantize_x(0, 0, PAIRS, False)
+            if s == 4:
+                quantize_x(0, x_full, 0, 0, PAIRS, False)
                 for m0, width in PIECES:
                     second_product(0, m0, width, 0)
-            if s >= 6:
-                combine(s - 2, first_m0, first_width)
-        for k, (m0, width) in enumerate(PIECES):
-            if k > 0:
-                for i in range(4, 8):
-                    combine(i, m0, width)
-            quantize_x(1, m0, width, True)
+        zero_late = keep.tile([P, 1], F32, name="zero_late")
+        nc.scalar.activation(zero_late[:], turns[7][:, 0:1], ACT.Sqrt, scale=0.0)
+        for m0, width in PIECES:
+            if m0 == HALF:
+                prod_half = keep.tile([P, PACK, HALF], F32, name="prod_half")
+                for i in range(PACK, 2 * PACK):
+                    pick_product(i, prod_half, HALF, HALF)
+                for i in range(PACK, 2 * PACK):
+                    add_offsets(i, prod_half, x_half[1], HALF, HALF)
+            h = m0 // HALF
+            quantize_x(1, x_half[h], h * HALF, m0, width, True)
             second_product(1, m0, width, m0)
             finish(m0, width)

@@ -26,7 +26,7 @@ WINDOWS = 6
 ROUNDER = 1.5 * 2.0**23
 HALF = PAIRS // 2
 PIECES = [(0, 256), (256, 128), (384, 128)]
-CAST_ON_VECTOR = [[32, 64], [48, 0]]
+CAST_ON_VECTOR = [[64, 64], [64, 64]]
 
 
 def tile_list_groove_crosstalk_scores_kernel(
@@ -131,7 +131,7 @@ def tile_list_groove_crosstalk_scores_kernel(
         quantize_w1(0, 0, 1)
         cast_both(0, 1)
         load_w1(1, 1, "slot_w1")
-        quantize_w1(0, 1, 1)
+        quantize_w1(0, 1, 4)
         w2_s = keep.tile([P, 2, N], U8, name="w_bf01", align_bytes=64)
         nc.gpsimd.memset(w2_s[:].rearrange("p a n -> p (a n)").bitcast(I32), 0)
         for q in range(4):
@@ -159,7 +159,7 @@ def tile_list_groove_crosstalk_scores_kernel(
                         stop=(a == 1),
                     )
                 dst = windows[i % WINDOWS][:, h * BANK : (h + 1) * BANK]
-                if (i, h) in [(0, 1)]:
+                if (i, h) in []:
                     nc.vector.tensor_copy(out=dst, in_=bank[:])
                 else:
                     nc.scalar.copy(out=dst, in_=bank[:])
@@ -174,7 +174,10 @@ def tile_list_groove_crosstalk_scores_kernel(
                 op0=ALU.mult,
                 op1=ALU.add,
             )
-            whole[i] = ring.tile([P, PAIRS], U32, name="whole")
+            if i == 7:
+                whole[i] = keep.tile([P, PAIRS], U32, name="whole_last")
+            else:
+                whole[i] = ring.tile([P, PAIRS], U32, name="whole")
             nc.scalar.activation(whole[i][:], phase[i][:], ACT.Copy, bias=ROUNDER, scale=1.0)
 
         def cosine(i):
@@ -216,7 +219,7 @@ def tile_list_groove_crosstalk_scores_kernel(
         x_scales = {}
 
         def quantize_x(b, x_rows, rows_m0, m0, width, on_vector):
-            woven = keep.tile([P, width, PACK], BF16, name="woven%d" % width, align_bytes=64)
+            woven = keep.tile([P, width, PACK], BF16, name="woven%d_%d" % (b, m0), align_bytes=64)
             dst = woven[:].rearrange("p (c i) t -> p c t i", i=4)
             src = x_rows[:, :, m0 - rows_m0 : m0 - rows_m0 + width].rearrange("p t (c i) -> p c t i", i=4)
             if on_vector:
@@ -263,9 +266,8 @@ def tile_list_groove_crosstalk_scores_kernel(
                 nc.sync.dma_start(out=out_rows[:, n0 : n0 + per_bank, m0 : m0 + width], in_=score[:])
 
         prod_full = keep.tile([P, PACK, PAIRS], F32, name="prod_full")
-        x_full = keep.tile([P, PACK, PAIRS], BF16, name="x_full")
         prod_half = keep.tile([P, PACK, HALF], F32, name="prod_half")
-        x_half = [keep.tile([P, PACK, HALF], BF16, name="x_half%d" % h) for h in range(2)]
+        x_half = {1: keep.tile([P, PACK, HALF], BF16, name="x_half1")}
         first_product(0)
         first_product(1)
         for s in range(9):
@@ -276,10 +278,8 @@ def tile_list_groove_crosstalk_scores_kernel(
                 cosine(i)
                 if i < PACK:
                     pick_product(i, prod_full, 0, PAIRS)
-                    add_offsets(i, prod_full, x_full, 0, PAIRS)
                 else:
                     pick_product(i, prod_half, 0, HALF)
-                    add_offsets(i, prod_half, x_half[0], 0, HALF)
             if s in (1, 2):
                 cast_both(1, s - 1)
                 quantize_w1(1, s - 1, 1)
@@ -290,9 +290,15 @@ def tile_list_groove_crosstalk_scores_kernel(
             if s + 2 < 8:
                 first_product(s + 2)
             if s == 4:
+                x_full = keep.tile([P, PACK, PAIRS], BF16, name="turn3")
+                for i in range(PACK):
+                    add_offsets(i, prod_full, x_full, 0, PAIRS)
                 quantize_x(0, x_full, 0, 0, PAIRS, False)
                 for m0, width in PIECES:
                     second_product(0, m0, width, 0)
+        x_half[0] = keep.tile([P, PACK, HALF], BF16, name="whole_last")
+        for i in range(PACK, 2 * PACK):
+            add_offsets(i, prod_half, x_half[0], 0, HALF)
         zero_late = keep.tile([P, 1], F32, name="zero_late")
         nc.scalar.activation(zero_late[:], turns[7][:, 0:1], ACT.Sqrt, scale=0.0)
         for m0, width in PIECES:

import math
from contextlib import ExitStack

import concourse.mybir as mybir

K, T, S, H, PAIRS, N = 1024, 4096, 1024, 1024, 512, 512
FLOPS = 2 * K * H * S + 2 * H * N * PAIRS

F32 = mybir.dt.float32
BF16 = mybir.dt.bfloat16
I32 = mybir.dt.int32
U32 = mybir.dt.uint32
U16 = mybir.dt.uint16
U8 = mybir.dt.uint8
FP8X4 = mybir.dt.float8_e4m3fn_x4
FP4X4 = mybir.dt.float4_e2m1fn_x4
ALU = mybir.AluOpType
ACT = mybir.ActivationFunctionType

P = 128
PACK = 4
K_PASS = P * PACK
BANK = 512
WINDOW = 2 * S
WINDOWS = 6
ROUNDER = 1.5 * 2.0**23
HALF = PAIRS // 2
PIECES = [(0, 256), (256, 128), (384, 128)]
CAST_ON_VECTOR = [[64, 64], [64, 64]]


def tile_list_groove_crosstalk_scores_kernel(
    tc, tab_words, tab_scales, offs, pos1, pos2, w1, gain, ecc, w2_words, w2_scales, out
):
    nc = tc.nc
    with ExitStack() as ctx:
        lists = ctx.enter_context(tc.tile_pool(name="lists", bufs=1))
        keep = ctx.enter_context(tc.tile_pool(name="keep", bufs=1))
        ring = ctx.enter_context(tc.tile_pool(name="ring", bufs=3))
        pair = ctx.enter_context(tc.tile_pool(name="pair", bufs=2))
        psum1 = ctx.enter_context(tc.psum_pool(name="psum1", bufs=4))
        psum2 = ctx.enter_context(tc.psum_pool(name="psum2", bufs=1))

        offs_t = lists.tile([P, S // 16], U16, name="offs_t")
        pos1_t = lists.tile([P, PAIRS // 16], U16, name="pos1_t")
        pos2_t = lists.tile([P, PAIRS // 16], U16, name="pos2_t")

        tab_w = [keep.tile([P, T], U16, name="slot_tab%d" % a) for a in range(2)]
        tab_s = keep.tile([P, T], U8, name="tab_s")
        picked_s = keep.tile([P, S], U8, name="picked_s")
        v_words = [keep.tile([P, S], U16, name="v_words%d" % a, align_bytes=64) for a in range(2)]
        v_scales = keep.tile([P, 2, S], U8, name="v_scales", align_bytes=64)
        w_raw = {}
        w_bf = {}
        w_codes = {}
        w_scales = {}
        for b in range(2):
            for a in range(2):
                w_bf[b, a] = keep.tile([P, PACK, P, PACK], BF16, name="w_bf%d%d" % (b, a), align_bytes=64)
                w_codes[b, a] = keep.tile([P, K_PASS], U32, name="w_codes%d%d" % (b, a), align_bytes=64)
                w_scales[b, a] = keep.tile([P, K_PASS], U8, name="w_scales%d%d" % (b, a), align_bytes=64)
        windows = [keep.tile([P, WINDOW], F32, name="window%d" % i) for i in range(WINDOWS)]
        ecc_t = {}
        turns = [keep.tile([P, PAIRS], F32, name="turn%d" % i) for i in range(8)]
        zero_in = keep.tile([P, 1], F32, name="zero_in")
        zero_bias = keep.tile([P, 1], F32, name="zero_bias")

        nc.vector.memset(tab_s[64:128, :].bitcast(I32), 0)
        nc.gpsimd.memset(zero_in[:], 0.0)
        nc.gpsimd.memset(tab_s[32:64, :].bitcast(I32), 0)
        nc.scalar.activation(zero_bias[:], zero_in[:], ACT.Sin)
        nc.gpsimd.memset(v_scales[:].rearrange("p a s -> p (a s)").bitcast(I32), 0)

        def load_w1(b, a, slot):
            rows = w1[a * K_PASS : (a + 1) * K_PASS, b * K_PASS : (b + 1) * K_PASS]
            w_raw[b, a] = keep.tile([P, PACK, K_PASS], F32, name=slot)
            nc.sync.dma_start(out=w_raw[b, a][:], in_=rows.rearrange("(p j) c -> p j c", j=PACK))

        def load_ecc(b, slot):
            rows = ecc[b * K_PASS : (b + 1) * K_PASS, :]
            ecc_t[b] = keep.tile([P, PACK, PAIRS], F32, name=slot)
            nc.sync.dma_start(out=ecc_t[b][:], in_=rows.rearrange("(p t) m -> p t m", t=PACK))

        nc.sync.dma_start(offs_t[:], offs)
        nc.sync.dma_start(out=tab_s[0:32, :].bitcast(I32), in_=tab_scales.rearrange("a g c -> g a c").bitcast(I32))
        nc.sync.dma_start(out=tab_w[0][:].bitcast(I32), in_=tab_words[0].bitcast(I32))
        load_w1(0, 0, "slot_w0")
        nc.sync.dma_start(out=tab_w[1][:].bitcast(I32), in_=tab_words[1].bitcast(I32))
        load_w1(0, 1, "slot_w1")
        nc.sync.dma_start(pos2_t[:], pos2)
        nc.sync.dma_start(pos1_t[:], pos1)

        def cast_w1(b, a, lo, hi, on_vector):
            dst = w_bf[b, a][:].rearrange("p t m j -> p m t j")[:, lo:hi, :, :]
            src = w_raw[b, a][:].rearrange("p j (m t) -> p m t j", t=PACK)[:, lo:hi, :, :]
            if on_vector:
                nc.vector.tensor_copy(out=dst, in_=src)
            else:
                nc.scalar.copy(out=dst, in_=src)

        def quantize_w1(b, a, parts):
            flat = w_bf[b, a][:].rearrange("p t m j -> p (t m j)")
            step = K_PASS // parts
            for c in range(0, K_PASS, step):
                nc.vector.quantize_mx(
                    out=w_codes[b, a][:, c : c + step].bitcast(FP8X4),
                    scales=w_scales[b, a][:, c : c + step],
                    in_=flat[:, PACK * c : PACK * (c + step)],
                )

        def cast_both(b, a):
            split = P - CAST_ON_VECTOR[b][a]
            cast_w1(b, a, 0, split // 2, False)
            cast_w1(b, a, split // 2, split, False)
            if split < P:
                cast_w1(b, a, split, P, True)

        nc.vector.tensor_copy(out=picked_s[:], in_=tab_s[:].indirect(offs_t[:]))
        for q in range(4):
            nc.scalar.dma_start(
                out=v_scales[32 * q : 32 * q + 4, :, :].bitcast(I32),
                in_=picked_s[8 * q : 8 * q + 8, :].bitcast(I32),
            )
        nc.vector.tensor_copy(out=v_words[0][:], in_=tab_w[0][:].indirect(offs_t[:]))
        load_w1(1, 0, "slot_tab0")
        cast_both(0, 0)
        gain_t = keep.tile([P, 2, PACK], F32, name="slot_w0")
        nc.sync.dma_start(out=gain_t[:], in_=gain.rearrange("(b p t) -> p b t", b=2, t=PACK))
        nc.vector.tensor_copy(out=v_words[1][:], in_=tab_w[1][:].indirect(offs_t[:]))
        load_ecc(0, "slot_tab1")
        quantize_w1(0, 0, 1)
        cast_both(0, 1)
        load_w1(1, 1, "slot_w1")
        quantize_w1(0, 1, 4)
        w2_s = keep.tile([P, 2, N], U8, name="w_bf01", align_bytes=64)
        nc.gpsimd.memset(w2_s[:].rearrange("p a n -> p (a n)").bitcast(I32), 0)
        for q in range(4):
            nc.sync.dma_start(
                out=w2_s[32 * q : 32 * q + 4, :, :].bitcast(I32),
                in_=w2_scales[:, 4 * q : 4 * q + 4, :].rearrange("a r c -> r a c").bitcast(I32),
            )

        phase = {}
        whole = {}

        def first_product(i):
            b, t = divmod(i, PACK)
            cols = slice(t * P, (t + 1) * P)
            for h in range(2):
                bank = psum1.tile([P, BANK], F32, name="bank")
                for a in range(2):
                    nc.tensor.matmul_mx(
                        out=bank[:],
                        lhsT=w_codes[b, a][:, cols].bitcast(FP8X4),
                        lhsT_scale=w_scales[b, a][:, cols],
                        rhs=v_words[a][:, h * BANK : (h + 1) * BANK].bitcast(FP4X4),
                        rhs_scale=v_scales[:, a, h * BANK : (h + 1) * BANK],
                        start=(a == 0),
                        stop=(a == 1),
                    )
                dst = windows[i % WINDOWS][:, h * BANK : (h + 1) * BANK]
                if (i, h) in []:
                    nc.vector.tensor_copy(out=dst, in_=bank[:])
                else:
                    nc.scalar.copy(out=dst, in_=bank[:])

        def pick_phase(i):
            phase[i] = ring.tile([P, PAIRS], F32, name="phase")
            nc.vector.tensor_scalar(
                out=phase[i][:],
                in0=windows[i % WINDOWS][:].indirect(pos2_t[:]),
                scalar1=1.0 / (2.0 * math.pi),
                scalar2=0.25,
                op0=ALU.mult,
                op1=ALU.add,
            )
            if i == 7:
                whole[i] = keep.tile([P, PAIRS], U32, name="whole_last")
            else:
                whole[i] = ring.tile([P, PAIRS], U32, name="whole")
            nc.scalar.activation(whole[i][:], phase[i][:], ACT.Copy, bias=ROUNDER, scale=1.0)

        def cosine(i):
            rest = ring.tile([P, PAIRS], F32, name="rest")
            nc.vector.scalar_tensor_tensor(
                out=rest[:],
                in0=whole[i][:].bitcast(I32),
                scalar=ROUNDER,
                in1=phase[i][:],
                op0=ALU.subtract,
                op1=ALU.subtract,
            )
            nc.scalar.activation(turns[i][:], rest[:], ACT.Sin, bias=zero_bias[:], scale=-2.0 * math.pi)

        def pick_product(i, prod, m0, width):
            if width == PAIRS:
                picks = pos1_t[:]
            else:
                picks = pos1_t[:, m0 // 16 : (m0 + width) // 16]
            nc.vector.tensor_tensor(
                out=prod[:, i % PACK, :],
                in0=windows[i % WINDOWS][:].indirect(picks),
                in1=turns[i][:, m0 : m0 + width],
                op=ALU.mult,
            )

        def add_offsets(i, prod, x_rows, m0, width):
            b, t = divmod(i, PACK)
            nc.vector.scalar_tensor_tensor(
                out=x_rows[:, t, :],
                in0=prod[:, t, :],
                scalar=gain_t[:, b, t : t + 1],
                in1=ecc_t[b][:, t, m0 : m0 + width],
                op0=ALU.mult,
                op1=ALU.add,
            )

        x_codes = {}
        x_scales = {}

        def quantize_x(b, x_rows, rows_m0, m0, width, on_vector):
            woven = keep.tile([P, width, PACK], BF16, name="woven%d_%d" % (b, m0), align_bytes=64)
            dst = woven[:].rearrange("p (c i) t -> p c t i", i=4)
            src = x_rows[:, :, m0 - rows_m0 : m0 - rows_m0 + width].rearrange("p t (c i) -> p c t i", i=4)
            if on_vector:
                nc.vector.tensor_copy(out=dst, in_=src)
            else:
                nc.scalar.copy(out=dst, in_=src)
            x_codes[b, m0] = keep.tile([P, width], U32, name="x_codes%d_%d" % (b, m0), align_bytes=64)
            x_scales[b, m0] = keep.tile([P, width], U8, name="x_scales%d_%d" % (b, m0), align_bytes=64)
            nc.vector.quantize_mx(
                out=x_codes[b, m0][:].bitcast(FP8X4),
                scales=x_scales[b, m0][:],
                in_=woven[:].rearrange("p m t -> p (m t)"),
            )

        sums = {}

        def second_product(b, m0, width, base):
            per_bank = BANK // width
            for n0 in range(0, N // P, per_bank):
                if b == 0:
                    sums[m0, n0] = psum2.tile([P, per_bank, width], F32, name="sums%d_%d" % (m0, n0))
                steps = [(n, c) for n in range(per_bank) for c in range(0, width, P)]
                for n, c in steps:
                    cols = slice(m0 - base + c, m0 - base + c + P)
                    nc.tensor.matmul_mx(
                        out=sums[m0, n0][:, n, c : c + P],
                        lhsT=w2_w[:, b, 2 * P * (n0 + n) : 2 * P * (n0 + n + 1)].bitcast(FP4X4),
                        lhsT_scale=w2_s[:, b, P * (n0 + n) : P * (n0 + n + 1)],
                        rhs=x_codes[b, base][:, cols].bitcast(FP8X4),
                        rhs_scale=x_scales[b, base][:, cols],
                        start=(b == 0 and (n, c) == steps[0]),
                        stop=(b == 1 and (n, c) == steps[-1]),
                    )

        out_rows = out.rearrange("(n p) m -> p n m", p=P)

        def finish(m0, width):
            per_bank = BANK // width
            for n0 in range(0, N // P, per_bank):
                size = pair.tile([P, per_bank, width], F32, name="size")
                nc.scalar.activation(size[:], sums[m0, n0][:], ACT.Abs, bias=zero_late[:])
                score = ring.tile([P, per_bank, width], F32, name="score")
                nc.scalar.activation(score[:], size[:], ACT.Sqrt, bias=0.2)
                nc.sync.dma_start(out=out_rows[:, n0 : n0 + per_bank, m0 : m0 + width], in_=score[:])

        prod_full = keep.tile([P, PACK, PAIRS], F32, name="prod_full")
        prod_half = keep.tile([P, PACK, HALF], F32, name="prod_half")
        x_half = {1: keep.tile([P, PACK, HALF], BF16, name="x_half1")}
        first_product(0)
        first_product(1)
        for s in range(9):
            if s < 8:
                pick_phase(s)
            if s >= 1:
                i = s - 1
                cosine(i)
                if i < PACK:
                    pick_product(i, prod_full, 0, PAIRS)
                else:
                    pick_product(i, prod_half, 0, HALF)
            if s in (1, 2):
                cast_both(1, s - 1)
                quantize_w1(1, s - 1, 1)
            if s == 1:
                load_ecc(1, "slot_tab0")
                w2_w = keep.tile([P, 2, 2 * N], U8, name="w_bf10", align_bytes=64)
                nc.sync.dma_start(out=w2_w[:].bitcast(I32), in_=w2_words.rearrange("a p c -> p a c").bitcast(I32))
            if s + 2 < 8:
                first_product(s + 2)
            if s == 4:
                x_full = keep.tile([P, PACK, PAIRS], BF16, name="turn3")
                for i in range(PACK):
                    add_offsets(i, prod_full, x_full, 0, PAIRS)
                quantize_x(0, x_full, 0, 0, PAIRS, False)
                for m0, width in PIECES:
                    second_product(0, m0, width, 0)
        x_half[0] = keep.tile([P, PACK, HALF], BF16, name="whole_last")
        for i in range(PACK, 2 * PACK):
            add_offsets(i, prod_half, x_half[0], 0, HALF)
        zero_late = keep.tile([P, 1], F32, name="zero_late")
        nc.scalar.activation(zero_late[:], turns[7][:, 0:1], ACT.Sqrt, scale=0.0)
        for m0, width in PIECES:
            if m0 == HALF:
                prod_half = keep.tile([P, PACK, HALF], F32, name="prod_half")
                for i in range(PACK, 2 * PACK):
                    pick_product(i, prod_half, HALF, HALF)
                for i in range(PACK, 2 * PACK):
                    add_offsets(i, prod_half, x_half[1], HALF, HALF)
            h = m0 // HALF
            quantize_x(1, x_half[h], h * HALF, m0, width, True)
            second_product(1, m0, width, m0)
            finish(m0, width)
